import numpy as np
import ml_dtypes


def mxq(x, axis, fmt="e4m3"):
    dtype, down = {"e4m3": (ml_dtypes.float8_e4m3fn, 7), "e5m2": (ml_dtypes.float8_e5m2, 14)}[fmt]
    v = np.moveaxis(np.asarray(x, np.float32).astype(ml_dtypes.bfloat16).astype(np.float64), axis, -1)
    blocks = v.reshape(v.shape[:-1] + (-1, 32))
    amax = np.abs(blocks).max(-1, keepdims=True)
    byte = np.maximum(np.where(amax > 0, np.frexp(amax)[1] - 1 + 127, 0) - down, 1)
    scale = np.exp2(byte - 127.0)
    codes = (blocks / scale).astype(np.float32).astype(dtype).astype(np.float64)
    return np.moveaxis((codes * scale).reshape(v.shape), -1, axis)


WIDE = False


def mx_kscale(k):
    if not WIDE:
        return np.ones(k)
    levels = np.array([24, -24, 12, -12, 0])
    if k % 512:
        return np.exp2(np.random.permutation(np.resize(levels, k // 32))).repeat(32)
    a = np.empty((k // 512, 16))
    for p in range(k // 512):
        a[p, :8] = np.random.permutation(np.resize(levels, 8))
        for g in range(8):
            far = levels[np.abs(levels - a[p, g]) >= 10]
            a[p, g + 8] = far[np.random.randint(len(far))]
    return np.exp2(a.ravel()).repeat(32)


def f64(x):
    return np.asarray(x).astype(np.float64)


def striped(idx):
    return np.tile(idx.reshape(-1, 16).T, (8, 1)).astype(np.uint16)


def unstriped(offs):
    return offs[:16].T.reshape(-1).astype(np.int64)


E2M1 = np.array([0.0, 0.5, 1.0, 1.5, 2.0, 3.0, 4.0, 6.0, -0.0, -0.5, -1.0, -1.5, -2.0, -3.0, -4.0, -6.0])


def pack_weight(w, fmt):
    k, n = w.shape
    w = f64(np.asarray(w, np.float32).astype(ml_dtypes.bfloat16)).reshape(k // 32, 32, n)
    amax = np.abs(w).max(1)
    if fmt == "e4m3":
        byte = np.frexp(amax)[1] - 1 + 127 - 7
    else:
        mant, ex = np.frexp(amax / 6.0)
        byte = np.where(mant > 0.5, ex, ex - 1) + 127
    byte = np.clip(np.where(amax > 0, byte, 1), 1, 254)
    scaled = (w * np.exp2(127.0 - byte)[:, None, :]).reshape(k, n).astype(np.float32)
    by_word = np.ascontiguousarray(scaled.reshape(k // 512, 128, 4, n).transpose(0, 1, 3, 2))
    if fmt == "e4m3":
        words = by_word.astype(ml_dtypes.float8_e4m3fn).view(np.uint8)
    else:
        c = by_word.astype(ml_dtypes.float4_e2m1fn).view(np.uint8) & 0xF
        words = (c[..., 0::2] | (c[..., 1::2] << 4)).reshape(k // 512, 128, 2 * n)
    return np.ascontiguousarray(words), np.ascontiguousarray(byte.astype(np.uint8).reshape(k // 512, 16, n))


def unpack_weight(words, scales, fmt):
    g, _, n = scales.shape
    words = np.ascontiguousarray(words).reshape(g, 128, n, -1)
    if fmt == "e4m3":
        vals = words.view(ml_dtypes.float8_e4m3fn).astype(np.float64)
    else:
        nib = np.empty((g, 128, n, 4), np.uint8)
        nib[..., 0::2] = words & 0xF
        nib[..., 1::2] = words >> 4
        vals = E2M1[nib]
    vals = vals * np.repeat(np.exp2(scales.astype(np.float64) - 127.0), 8, axis=1)[..., None]
    return vals.transpose(0, 1, 3, 2).reshape(g * 512, n)


def pack_table4(v):
    words, scales = pack_weight(v, "e2m1")
    g, t = words.shape[0] // 2, v.shape[1]
    return np.ascontiguousarray(words.reshape(g, 2, 128, t, 2).transpose(0, 2, 3, 1, 4).reshape(g, 128, t, 4)), scales


def unpack_table4(words, scales):
    g, _, t, _ = words.shape
    return unpack_weight(words.reshape(g, 128, t, 2, 2).transpose(0, 3, 1, 2, 4).reshape(2 * g, 128, 2 * t), scales, "e2m1")


def split(x):
    m, e = np.frexp(f64(x))
    hi = np.ldexp(np.trunc(16.0 * m) / 16.0, e)
    return hi, f64(x) - hi


K, N, T, J = 1024, 512, 2048, 1024


def setup_inputs():
    n = np.random.standard_normal
    s = mx_kscale(K)[:, None]
    p_tab = pack_table4(n((K, T)) * s)
    p_tab2 = pack_table4(n((K, T)) * s)
    p_wi = pack_weight(n((K, N)) / np.sqrt(2 * K) / s, "e4m3")
    return {
        "tab_words": p_tab[0],
        "tab_scales": p_tab[1],
        "tab2_words": p_tab2[0],
        "tab2_scales": p_tab2[1],
        "wr": (n((K, N)) / np.sqrt(2 * K) / s).astype(np.float32),
        "wi_words": p_wi[0],
        "wi_scales": p_wi[1],
        "offs": striped(np.random.permutation(T)[:J]),
    }


def reference(tab_words, tab_scales, tab2_words, tab2_scales, wr, wi_words, wi_scales, offs):
    idx = unstriped(offs)
    tab_ = unpack_table4(tab_words, tab_scales)[:, idx]
    tab2_ = unpack_table4(tab2_words, tab2_scales)[:, idx]
    wr_hi, wr_lo = split(wr)
    wr_hi_, wr_lo_ = mxq(wr_hi, 0, "e4m3"), mxq(wr_lo, 0, "e4m3")
    wi_ = unpack_weight(wi_words, wi_scales, "e4m3")
    rr = wr_hi_.T @ tab_ + wr_lo_.T @ tab_
    ii = wi_.T @ tab2_
    zr = rr - ii
    ri = wr_hi_.T @ tab2_ + wr_lo_.T @ tab2_ + wi_.T @ tab_
    zi = ri
    return np.sqrt((zr) ** 2 + (zi) ** 2)

@@ -1,0 +1,269 @@
+from contextlib import ExitStack
+
+import concourse.mybir as mybir
+
+K, N, T, J = 1024, 512, 2048, 1024
+FLOPS = 6 * 2 * K * N * J
+
+F32 = mybir.dt.float32
+BF16 = mybir.dt.bfloat16
+I32 = mybir.dt.int32
+U32 = mybir.dt.uint32
+U16 = mybir.dt.uint16
+U8 = mybir.dt.uint8
+FP8X4 = mybir.dt.float8_e4m3fn_x4
+FP4X4 = mybir.dt.float4_e2m1fn_x4
+ALU = mybir.AluOpType
+ACT = mybir.ActivationFunctionType
+
+P = 128
+PACK = 4
+PASSES = 2
+JT = 512
+NH = 256
+HI_MASK = -983056
+SHIFT = 4
+SHIFT_ROWS = 112
+
+
+def tile_list_cpxtab_hl_mag_kernel(
+    tc, tab_words, tab_scales, tab2_words, tab2_scales, wr, wi_words, wi_scales, offs, out
+):
+    nc = tc.nc
+    with ExitStack() as ctx:
+        keep = ctx.enter_context(tc.tile_pool(name="keep", bufs=1))
+        work = ctx.enter_context(tc.tile_pool(name="work", bufs=3))
+        psum = ctx.enter_context(tc.psum_pool(name="psum", bufs=8))
+
+        offsets = keep.tile([P, J // 16], U16, name="offsets")
+        nc.sync.dma_start(offsets[:], offs)
+
+        RE, IM = 0, 1
+        words_hbm = [tab_words, tab2_words]
+        scales_hbm = [tab_scales, tab2_scales]
+        word_win = [keep.tile([P, T], I32, name="word_win%d" % v, align_bytes=64) for v in range(2)]
+        scale_win = [keep.tile([P, T // 4], I32, name="scale_win%d" % v, align_bytes=64) for v in range(2)]
+        wi_codes = keep.tile([P, PASSES, N], I32, name="wi_codes", align_bytes=64)
+        wi_plane = keep.tile([P, PASSES, N // 4], I32, name="wi_plane", align_bytes=64)
+        moved = keep.tile([P, 2, J // 4], I32, name="moved", align_bytes=64)
+        wr_raw = {}
+
+        def load_scales(v):
+            for q in range(4):
+                nc.sync.dma_start(
+                    scale_win[v][32 * q : 32 * q + 8, :],
+                    scales_hbm[v][:, 4 * q : 4 * q + 4, :].bitcast(I32),
+                )
+
+        def load_words(v):
+            nc.sync.dma_start(word_win[v][:], words_hbm[v][0].rearrange("p t b -> p (t b)").bitcast(I32))
+
+        def load_wr(a, h):
+            wr_raw[a, h] = keep.tile([P, PACK, NH], F32, name="wr_raw%d%d" % (a, h))
+            rows = wr[512 * a : 512 * (a + 1), NH * h : NH * (h + 1)]
+            nc.sync.dma_start(wr_raw[a, h][:], rows.rearrange("(p i) n -> p i n", i=PACK))
+
+        nc.vector.memset(scale_win[IM][:], 0)
+        nc.vector.memset(wi_plane[:], 0)
+        nc.vector.memset(moved[:], 0)
+        nc.vector.memset(scale_win[RE][:], 0)
+        load_scales(IM)
+        load_words(IM)
+        nc.sync.dma_start(wi_codes[:], wi_words.rearrange("a p n i -> p a (n i)").bitcast(I32))
+        for q in range(4):
+            nc.sync.dma_start(
+                wi_plane[32 * q : 32 * q + 4, :, :],
+                wi_scales[:, 4 * q : 4 * q + 4, :].rearrange("a r n -> r a n").bitcast(I32),
+            )
+        load_wr(0, 0)
+        load_scales(RE)
+        load_words(RE)
+        load_wr(1, 0)
+        load_wr(0, 1)
+        load_wr(1, 1)
+
+        planes = {}
+        codes = {}
+        picked = {}
+
+        def gather_scales(v):
+            both = keep.tile([P, J], U8, name="both%d" % v, align_bytes=64)
+            nc.vector.tensor_copy(both[:], scale_win[v][:].bitcast(U8).indirect(offsets[:]))
+            dst = moved[:, v, :]
+            nc.scalar.dma_start(dst[0:SHIFT_ROWS, :], both[SHIFT : SHIFT + SHIFT_ROWS, :].bitcast(I32))
+            for jt in range(2):
+                cols = slice(jt * JT, (jt + 1) * JT)
+                planes[v, jt] = [both[:, cols], dst.bitcast(U8)[:, cols]]
+
+        def gather_words(v, jt):
+            picked[v, jt] = keep.tile([P, JT], U32, name="picked%d%d" % (v, jt), align_bytes=64)
+            lst = offsets[:, jt * (JT // 16) : (jt + 1) * (JT // 16)]
+            nc.vector.tensor_copy(picked[v, jt][:], word_win[v][:].bitcast(U32).indirect(lst))
+
+        def part_words(v, jt):
+            codes[v, jt] = keep.tile([P, PASSES, 2 * JT], U8, name="codes%d%d" % (v, jt), align_bytes=64)
+            nc.vector.tensor_copy(
+                codes[v, jt][:].bitcast(U16),
+                picked[v, jt][:].bitcast(U16).rearrange("p (j d) -> p d j", d=PASSES),
+            )
+
+        hi_bf = {}
+        lo_bf = {}
+        upper = {}
+        wq = {}
+
+        def upper_halves(a, h):
+            upper[a, h] = keep.tile([P, NH, PACK], BF16, name="upper%d%d" % (a, h), align_bytes=64)
+            halves = wr_raw[a, h][:].bitcast(BF16).rearrange("p i (n e) -> p n i e", e=2)
+            nc.scalar.copy(upper[a, h][:], halves[:, :, :, 1])
+
+        def mask_hi(a, h):
+            hi_bf[a, h] = keep.tile([P, NH * PACK], BF16, name="hi%d%d" % (a, h), align_bytes=64)
+            nc.vector.tensor_scalar(
+                hi_bf[a, h][:].bitcast(I32),
+                upper[a, h][:].rearrange("p n i -> p (n i)").bitcast(I32),
+                HI_MASK,
+                None,
+                ALU.bitwise_and,
+            )
+
+        def make_lo(a, h):
+            lo_bf[a, h] = keep.tile([P, NH * PACK], BF16, name="lo%d%d" % (a, h), align_bytes=64)
+            nc.vector.tensor_tensor(
+                lo_bf[a, h][:].rearrange("p (n i) -> p n i", i=PACK),
+                wr_raw[a, h][:].rearrange("p i n -> p n i"),
+                hi_bf[a, h][:].rearrange("p (n i) -> p n i", i=PACK),
+                ALU.subtract,
+            )
+
+        def quantise(part, a, h):
+            src = hi_bf if part == "hi" else lo_bf
+            c = keep.tile([P, NH], U32, name="c%s%d%d" % (part, a, h), align_bytes=64)
+            s = keep.tile([P, NH], U8, name="s%s%d%d" % (part, a, h), align_bytes=64)
+            nc.vector.quantize_mx(c[:].bitcast(FP8X4), s[:], src[a, h][:])
+            wq[part, a, h] = (c, s)
+
+        banks = {}
+        done = {}
+        TOTAL = {"ii": 2, "rr": 4, "ri": 6}
+
+        def mm(group, part, v, a, nt, jt):
+            key = (group, nt, jt)
+            if key not in banks:
+                banks[key] = psum.tile([P, JT], F32, name="acc")
+                done[key] = 0
+            if part == "wi":
+                w = wi_codes[:, a, nt * P : (nt + 1) * P]
+                ws = wi_plane[:, a, :].bitcast(U8)[:, nt * P : (nt + 1) * P]
+            else:
+                c, s = wq[part, a, nt // 2]
+                w = c[:, (nt % 2) * P : (nt % 2 + 1) * P]
+                ws = s[:, (nt % 2) * P : (nt % 2 + 1) * P]
+            nc.tensor.matmul_mx(
+                banks[key][:],
+                lhsT=w.bitcast(FP8X4),
+                lhsT_scale=ws,
+                rhs=codes[v, jt][:, a, :].bitcast(FP4X4),
+                rhs_scale=planes[v, jt][a],
+                start=(done[key] == 0),
+                stop=(done[key] == TOTAL[group] - 1),
+            )
+            done[key] += 1
+
+        ii_sb = {}
+        zr_sq = {}
+
+        def take_ii(nt, jt):
+            ii_sb[nt, jt] = keep.tile([P, JT], F32, name="ii%d%d" % (nt, jt))
+            nc.scalar.copy(ii_sb[nt, jt][:], banks["ii", nt, jt][:])
+
+        def take_rr(nt, jt):
+            zr = work.tile([P, JT], F32, name="zr")
+            nc.vector.tensor_tensor(zr[:], banks["rr", nt, jt][:], ii_sb[nt, jt][:], ALU.subtract)
+            zr_sq[nt, jt] = work.tile([P, JT], F32, name="zr_sq")
+            nc.scalar.activation(zr_sq[nt, jt][:], zr[:], ACT.Square)
+
+        def finish(nt, jt):
+            zi_sq = work.tile([P, JT], F32, name="zi_sq")
+            nc.scalar.activation(zi_sq[:], banks["ri", nt, jt][:], ACT.Square)
+            total = work.tile([P, JT], F32, name="total")
+            nc.vector.tensor_tensor(total[:], zi_sq[:], zr_sq[nt, jt][:], ALU.add)
+            mag = work.tile([P, JT], F32, name="mag")
+            nc.scalar.activation(mag[:], total[:], ACT.Sqrt)
+            nc.sync.dma_start(out[nt * P : (nt + 1) * P, jt * JT : (jt + 1) * JT], mag[:])
+
+        def ii_tiles(jt):
+            for a in range(PASSES):
+                for nt in range(4):
+                    mm("ii", "wi", IM, a, nt, jt)
+            for nt in range(4):
+                take_ii(nt, jt)
+
+        def hilo(group, v, a, nt, jt):
+            mm(group, "hi", v, a, nt, jt)
+            mm(group, "lo", v, a, nt, jt)
+
+        gather_scales(IM)
+        gather_words(IM, 0)
+        part_words(IM, 0)
+        ii_tiles(0)
+        upper_halves(0, 0)
+        gather_words(IM, 1)
+        mask_hi(0, 0)
+        part_words(IM, 1)
+        upper_halves(1, 0)
+        ii_tiles(1)
+        make_lo(0, 0)
+        quantise("hi", 0, 0)
+        quantise("lo", 0, 0)
+        gather_scales(RE)
+        gather_words(RE, 0)
+        part_words(RE, 0)
+        mask_hi(1, 0)
+        for jt in range(2):
+            for nt in range(2):
+                hilo("ri", IM, 0, nt, jt)
+        for nt in range(2):
+            hilo("rr", RE, 0, nt, 0)
+            for a in range(PASSES):
+                mm("ri", "wi", RE, a, nt, 0)
+        make_lo(1, 0)
+        quantise("hi", 1, 0)
+        quantise("lo", 1, 0)
+        upper_halves(0, 1)
+        upper_halves(1, 1)
+        gather_words(RE, 1)
+        mask_hi(0, 1)
+        part_words(RE, 1)
+        for nt in range(2):
+            hilo("rr", RE, 1, nt, 0)
+            hilo("ri", IM, 1, nt, 0)
+        make_lo(0, 1)
+        quantise("hi", 0, 1)
+        mask_hi(1, 1)
+        quantise("lo", 0, 1)
+        for nt in range(2):
+            take_rr(nt, 0)
+            finish(nt, 0)
+        for nt in range(2):
+            hilo("ri", IM, 1, nt, 1)
+        make_lo(1, 1)
+        quantise("hi", 1, 1)
+        quantise("lo", 1, 1)
+        for nt in range(2):
+            for a in range(PASSES):
+                hilo("rr", RE, a, nt, 1)
+            for a in range(PASSES):
+                mm("ri", "wi", RE, a, nt, 1)
+            take_rr(nt, 1)
+            finish(nt, 1)
+        for jt in range(2):
+            for nt in range(2, 4):
+                for a in range(PASSES):
+                    hilo("rr", RE, a, nt, jt)
+                for a in range(PASSES):
+                    mm("ri", "wi", RE, a, nt, jt)
+                for a in range(PASSES):
+                    hilo("ri", IM, a, nt, jt)
+                take_rr(nt, jt)
+                finish(nt, jt)

@@ -32,7 +32,8 @@ def tile_list_cpxtab_hl_mag_kernel(
     nc = tc.nc
     with ExitStack() as ctx:
         keep = ctx.enter_context(tc.tile_pool(name="keep", bufs=1))
-        work = ctx.enter_context(tc.tile_pool(name="work", bufs=3))
+        work = ctx.enter_context(tc.tile_pool(name="work", bufs=4))
+        stage = ctx.enter_context(tc.tile_pool(name="stage", bufs=2))
         psum = ctx.enter_context(tc.psum_pool(name="psum", bufs=8))
 
         offsets = keep.tile([P, J // 16], U16, name="offsets")
@@ -41,7 +42,7 @@ def tile_list_cpxtab_hl_mag_kernel(
         RE, IM = 0, 1
         words_hbm = [tab_words, tab2_words]
         scales_hbm = [tab_scales, tab2_scales]
-        word_win = [keep.tile([P, T], I32, name="word_win%d" % v, align_bytes=64) for v in range(2)]
+        word_win = {}
         scale_win = [keep.tile([P, T // 4], I32, name="scale_win%d" % v, align_bytes=64) for v in range(2)]
         wi_codes = keep.tile([P, PASSES, N], I32, name="wi_codes", align_bytes=64)
         wi_plane = keep.tile([P, PASSES, N // 4], I32, name="wi_plane", align_bytes=64)
@@ -55,48 +56,54 @@ def tile_list_cpxtab_hl_mag_kernel(
                     scales_hbm[v][:, 4 * q : 4 * q + 4, :].bitcast(I32),
                 )
 
-        def load_words(v):
-            nc.sync.dma_start(word_win[v][:], words_hbm[v][0].rearrange("p t b -> p (t b)").bitcast(I32))
+        def load_words(v, queue):
+            word_win[v] = keep.tile([P, T], I32, name="word_win", align_bytes=64)
+            queue.dma_start(word_win[v][:], words_hbm[v][0].rearrange("p t b -> p (t b)").bitcast(I32))
 
-        def load_wr(a, h):
-            wr_raw[a, h] = keep.tile([P, PACK, NH], F32, name="wr_raw%d%d" % (a, h))
+        def load_wr(a, h, queue):
+            wr_raw[a, h] = stage.tile([P, PACK, NH], F32, name="wr_raw")
             rows = wr[512 * a : 512 * (a + 1), NH * h : NH * (h + 1)]
-            nc.sync.dma_start(wr_raw[a, h][:], rows.rearrange("(p i) n -> p i n", i=PACK))
+            queue.dma_start(wr_raw[a, h][:], rows.rearrange("(p i) n -> p i n", i=PACK))
 
         nc.vector.memset(scale_win[IM][:], 0)
         nc.vector.memset(wi_plane[:], 0)
         nc.vector.memset(moved[:], 0)
         nc.vector.memset(scale_win[RE][:], 0)
+        zero_in = keep.tile([P, 1], F32, name="zero_in")
+        zero = keep.tile([P, 1], F32, name="zero")
+        nc.gpsimd.memset(zero_in[:], 0.0)
+
+        def load_wi(a):
+            nc.scalar.dma_start(wi_codes[:, a, :], wi_words[a].rearrange("p n i -> p (n i)").bitcast(I32))
+
+        load_words(IM, nc.scalar)
+        load_wi(0)
+        nc.scalar.activation(zero[:], zero_in[:], ACT.Sqrt)
         load_scales(IM)
-        load_words(IM)
-        nc.sync.dma_start(wi_codes[:], wi_words.rearrange("a p n i -> p a (n i)").bitcast(I32))
         for q in range(4):
             nc.sync.dma_start(
                 wi_plane[32 * q : 32 * q + 4, :, :],
                 wi_scales[:, 4 * q : 4 * q + 4, :].rearrange("a r n -> r a n").bitcast(I32),
             )
-        load_wr(0, 0)
+        load_wi(1)
+        load_wr(0, 0, nc.scalar)
+        load_wr(1, 0, nc.scalar)
         load_scales(RE)
-        load_words(RE)
-        load_wr(1, 0)
-        load_wr(0, 1)
-        load_wr(1, 1)
 
         planes = {}
         codes = {}
         picked = {}
 
-        def gather_scales(v):
-            both = keep.tile([P, J], U8, name="both%d" % v, align_bytes=64)
-            nc.vector.tensor_copy(both[:], scale_win[v][:].bitcast(U8).indirect(offsets[:]))
-            dst = moved[:, v, :]
-            nc.scalar.dma_start(dst[0:SHIFT_ROWS, :], both[SHIFT : SHIFT + SHIFT_ROWS, :].bitcast(I32))
-            for jt in range(2):
-                cols = slice(jt * JT, (jt + 1) * JT)
-                planes[v, jt] = [both[:, cols], dst.bitcast(U8)[:, cols]]
+        def gather_scales(v, jt):
+            both = keep.tile([P, JT], U8, name="both%d%d" % (v, jt), align_bytes=64)
+            lst = offsets[:, jt * (JT // 16) : (jt + 1) * (JT // 16)]
+            nc.vector.tensor_copy(both[:], scale_win[v][:].bitcast(U8).indirect(lst))
+            dst = moved[:, v, jt * (JT // 4) : (jt + 1) * (JT // 4)]
+            nc.sync.dma_start(dst[0:SHIFT_ROWS, :], both[SHIFT : SHIFT + SHIFT_ROWS, :].bitcast(I32))
+            planes[v, jt] = [both[:], dst.bitcast(U8)]
 
         def gather_words(v, jt):
-            picked[v, jt] = keep.tile([P, JT], U32, name="picked%d%d" % (v, jt), align_bytes=64)
+            picked[v, jt] = keep.tile([P, JT], U32, name="picked", align_bytes=64)
             lst = offsets[:, jt * (JT // 16) : (jt + 1) * (JT // 16)]
             nc.vector.tensor_copy(picked[v, jt][:], word_win[v][:].bitcast(U32).indirect(lst))
 
@@ -183,14 +190,23 @@ def tile_list_cpxtab_hl_mag_kernel(
             zr_sq[nt, jt] = work.tile([P, JT], F32, name="zr_sq")
             nc.scalar.activation(zr_sq[nt, jt][:], zr[:], ACT.Square)
 
-        def finish(nt, jt):
-            zi_sq = work.tile([P, JT], F32, name="zi_sq")
-            nc.scalar.activation(zi_sq[:], banks["ri", nt, jt][:], ACT.Square)
+        zi_sq = {}
+
+        def take_ri(nt, jt, pieces=1):
+            zi_sq[nt, jt] = work.tile([P, JT], F32, name="zi_sq")
+            w = JT // pieces
+            for c in range(0, JT, w):
+                nc.scalar.activation(zi_sq[nt, jt][:, c : c + w], banks["ri", nt, jt][:, c : c + w], ACT.Square)
+
+        def finish(nt, jt, pieces=1):
             total = work.tile([P, JT], F32, name="total")
-            nc.vector.tensor_tensor(total[:], zi_sq[:], zr_sq[nt, jt][:], ALU.add)
             mag = work.tile([P, JT], F32, name="mag")
-            nc.scalar.activation(mag[:], total[:], ACT.Sqrt)
-            nc.sync.dma_start(out[nt * P : (nt + 1) * P, jt * JT : (jt + 1) * JT], mag[:])
+            w = JT // pieces
+            for c in range(0, JT, w):
+                cols = slice(c, c + w)
+                nc.vector.tensor_tensor(total[:, cols], zi_sq[nt, jt][:, cols], zr_sq[nt, jt][:, cols], ALU.add)
+                nc.scalar.activation(mag[:, cols], total[:, cols], ACT.Sqrt, bias=zero[:])
+                nc.sync.dma_start(out[nt * P : (nt + 1) * P, jt * JT + c : jt * JT + c + w], mag[:, cols])
 
         def ii_tiles(jt):
             for a in range(PASSES):
@@ -203,67 +219,78 @@ def tile_list_cpxtab_hl_mag_kernel(
             mm(group, "hi", v, a, nt, jt)
             mm(group, "lo", v, a, nt, jt)
 
-        gather_scales(IM)
         gather_words(IM, 0)
+        gather_scales(IM, 0)
         part_words(IM, 0)
         ii_tiles(0)
         upper_halves(0, 0)
-        gather_words(IM, 1)
-        mask_hi(0, 0)
-        part_words(IM, 1)
         upper_halves(1, 0)
+        gather_words(IM, 1)
+        load_words(RE, nc.sync)
+        gather_scales(IM, 1)
+        part_words(IM, 1)
         ii_tiles(1)
+        mask_hi(0, 0)
+        mask_hi(1, 0)
         make_lo(0, 0)
+        load_wr(0, 1, nc.sync)
         quantise("hi", 0, 0)
         quantise("lo", 0, 0)
-        gather_scales(RE)
-        gather_words(RE, 0)
-        part_words(RE, 0)
-        mask_hi(1, 0)
-        for jt in range(2):
-            for nt in range(2):
-                hilo("ri", IM, 0, nt, jt)
-        for nt in range(2):
-            hilo("rr", RE, 0, nt, 0)
-            for a in range(PASSES):
-                mm("ri", "wi", RE, a, nt, 0)
         make_lo(1, 0)
+        load_wr(1, 1, nc.sync)
         quantise("hi", 1, 0)
         quantise("lo", 1, 0)
+        for a in range(PASSES):
+            for jt in range(2):
+                for nt in range(2):
+                    hilo("ri", IM, a, nt, jt)
         upper_halves(0, 1)
         upper_halves(1, 1)
-        gather_words(RE, 1)
-        mask_hi(0, 1)
-        part_words(RE, 1)
-        for nt in range(2):
-            hilo("rr", RE, 1, nt, 0)
-            hilo("ri", IM, 1, nt, 0)
-        make_lo(0, 1)
-        quantise("hi", 0, 1)
-        mask_hi(1, 1)
-        quantise("lo", 0, 1)
-        for nt in range(2):
-            take_rr(nt, 0)
-            finish(nt, 0)
-        for nt in range(2):
-            hilo("ri", IM, 1, nt, 1)
-        make_lo(1, 1)
-        quantise("hi", 1, 1)
-        quantise("lo", 1, 1)
-        for nt in range(2):
-            for a in range(PASSES):
-                hilo("rr", RE, a, nt, 1)
-            for a in range(PASSES):
-                mm("ri", "wi", RE, a, nt, 1)
-            take_rr(nt, 1)
-            finish(nt, 1)
         for jt in range(2):
-            for nt in range(2, 4):
-                for a in range(PASSES):
+            gather_words(RE, jt)
+            gather_scales(RE, jt)
+            part_words(RE, jt)
+            for a in range(PASSES):
+                for nt in range(2):
                     hilo("rr", RE, a, nt, jt)
+                    mm("ri", "wi", RE, a, nt, jt)
+            if jt == 1:
+                mask_hi(0, 1)
+                mask_hi(1, 1)
+                make_lo(0, 1)
+                quantise("hi", 0, 1)
+                quantise("lo", 0, 1)
+                for nt in range(2):
+                    take_rr(nt, 0)
+                    take_ri(nt, 0)
+                make_lo(1, 1)
+                quantise("hi", 1, 1)
+                quantise("lo", 1, 1)
+        for nt in range(2):
+            take_rr(nt, 1)
+            take_ri(nt, 1)
+        for jt in range(2):
+            for nt in range(2):
+                finish(nt, jt)
+        late = [(2, 0), (3, 0), (2, 1), (3, 1)]
+        for nt, jt in late[:-1]:
+            for a in range(PASSES):
+                mm("ri", "wi", RE, a, nt, jt)
+
+        def rr_group(nt, jt):
+            for a in range(PASSES):
+                hilo("rr", RE, a, nt, jt)
+            take_rr(nt, jt)
+
+        rr_group(*late[0])
+        for step, (nt, jt) in enumerate(late):
+            last = step == len(late) - 1
+            if last:
                 for a in range(PASSES):
                     mm("ri", "wi", RE, a, nt, jt)
-                for a in range(PASSES):
-                    hilo("ri", IM, a, nt, jt)
-                take_rr(nt, jt)
-                finish(nt, jt)
+            else:
+                rr_group(*late[step + 1])
+            for a in range(PASSES):
+                hilo("ri", IM, a, nt, jt)
+            take_ri(nt, jt, 2 if last else 1)
+            finish(nt, jt, 2 if last else 1)

@@ -103,7 +103,7 @@ def tile_list_cpxtab_hl_mag_kernel(
             planes[v, jt] = [both[:], dst.bitcast(U8)]
 
         def gather_words(v, jt):
-            picked[v, jt] = keep.tile([P, JT], U32, name="picked", align_bytes=64)
+            picked[v, jt] = keep.tile([P, JT], U32, name="picked%d%d" % (v, jt), align_bytes=64)
             lst = offsets[:, jt * (JT // 16) : (jt + 1) * (JT // 16)]
             nc.vector.tensor_copy(picked[v, jt][:], word_win[v][:].bitcast(U32).indirect(lst))
 
@@ -137,9 +137,9 @@ def tile_list_cpxtab_hl_mag_kernel(
         def make_lo(a, h):
             lo_bf[a, h] = keep.tile([P, NH * PACK], BF16, name="lo%d%d" % (a, h), align_bytes=64)
             nc.vector.tensor_tensor(
-                lo_bf[a, h][:].rearrange("p (n i) -> p n i", i=PACK),
-                wr_raw[a, h][:].rearrange("p i n -> p n i"),
-                hi_bf[a, h][:].rearrange("p (n i) -> p n i", i=PACK),
+                lo_bf[a, h][:].rearrange("p (c n i) -> p c i n", n=4, i=PACK),
+                wr_raw[a, h][:].rearrange("p i (c n) -> p c i n", n=4),
+                hi_bf[a, h][:].rearrange("p (c n i) -> p c i n", n=4, i=PACK),
                 ALU.subtract,
             )
 
@@ -272,25 +272,17 @@ def tile_list_cpxtab_hl_mag_kernel(
         for jt in range(2):
             for nt in range(2):
                 finish(nt, jt)
-        late = [(2, 0), (3, 0), (2, 1), (3, 1)]
-        for nt, jt in late[:-1]:
-            for a in range(PASSES):
-                mm("ri", "wi", RE, a, nt, jt)
-
-        def rr_group(nt, jt):
-            for a in range(PASSES):
-                hilo("rr", RE, a, nt, jt)
-            take_rr(nt, jt)
-
-        rr_group(*late[0])
-        for step, (nt, jt) in enumerate(late):
-            last = step == len(late) - 1
-            if last:
+        for jt in range(2):
+            for nt in range(2, 4):
                 for a in range(PASSES):
                     mm("ri", "wi", RE, a, nt, jt)
-            else:
-                rr_group(*late[step + 1])
-            for a in range(PASSES):
-                hilo("ri", IM, a, nt, jt)
-            take_ri(nt, jt, 2 if last else 1)
-            finish(nt, jt, 2 if last else 1)
+        for jt in range(2):
+            for nt in range(2, 4):
+                pieces = 2 if (jt, nt) == (1, 3) else 1
+                for a in range(PASSES):
+                    hilo("rr", RE, a, nt, jt)
+                for a in range(PASSES):
+                    hilo("ri", IM, a, nt, jt)
+                take_rr(nt, jt)
+                take_ri(nt, jt, pieces)
+                finish(nt, jt, pieces)

@@ -121,8 +121,8 @@ def tile_list_cpxtab_hl_mag_kernel(
 
         def upper_halves(a, h):
             upper[a, h] = keep.tile([P, NH, PACK], BF16, name="upper%d%d" % (a, h), align_bytes=64)
-            halves = wr_raw[a, h][:].bitcast(BF16).rearrange("p i (n e) -> p n i e", e=2)
-            nc.scalar.copy(upper[a, h][:], halves[:, :, :, 1])
+            halves = wr_raw[a, h][:].bitcast(BF16).rearrange("p i (c n e) -> p c i n e", n=4, e=2)
+            nc.scalar.copy(upper[a, h][:].rearrange("p (c n) i -> p c i n", n=4), halves[:, :, :, :, 1])
 
         def mask_hi(a, h):
             hi_bf[a, h] = keep.tile([P, NH * PACK], BF16, name="hi%d%d" % (a, h), align_bytes=64)

from contextlib import ExitStack

import concourse.mybir as mybir

K, N, T, J = 1024, 512, 2048, 1024
FLOPS = 6 * 2 * K * N * J

F32 = mybir.dt.float32
BF16 = mybir.dt.bfloat16
I32 = mybir.dt.int32
U32 = mybir.dt.uint32
U16 = mybir.dt.uint16
U8 = mybir.dt.uint8
FP8X4 = mybir.dt.float8_e4m3fn_x4
FP4X4 = mybir.dt.float4_e2m1fn_x4
ALU = mybir.AluOpType
ACT = mybir.ActivationFunctionType

P = 128
PACK = 4
PASSES = 2
JT = 512
NH = 256
HI_MASK = -983056
SHIFT = 4
SHIFT_ROWS = 112


def tile_list_cpxtab_hl_mag_kernel(
    tc, tab_words, tab_scales, tab2_words, tab2_scales, wr, wi_words, wi_scales, offs, out
):
    nc = tc.nc
    with ExitStack() as ctx:
        keep = ctx.enter_context(tc.tile_pool(name="keep", bufs=1))
        work = ctx.enter_context(tc.tile_pool(name="work", bufs=4))
        stage = ctx.enter_context(tc.tile_pool(name="stage", bufs=2))
        psum = ctx.enter_context(tc.psum_pool(name="psum", bufs=8))

        offsets = keep.tile([P, J // 16], U16, name="offsets")
        nc.sync.dma_start(offsets[:], offs)

        RE, IM = 0, 1
        words_hbm = [tab_words, tab2_words]
        scales_hbm = [tab_scales, tab2_scales]
        word_win = {}
        scale_win = [keep.tile([P, T // 4], I32, name="scale_win%d" % v, align_bytes=64) for v in range(2)]
        wi_codes = keep.tile([P, PASSES, N], I32, name="wi_codes", align_bytes=64)
        wi_plane = keep.tile([P, PASSES, N // 4], I32, name="wi_plane", align_bytes=64)
        moved = keep.tile([P, 2, J // 4], I32, name="moved", align_bytes=64)
        wr_raw = {}

        def load_scales(v):
            for q in range(4):
                nc.sync.dma_start(
                    scale_win[v][32 * q : 32 * q + 8, :],
                    scales_hbm[v][:, 4 * q : 4 * q + 4, :].bitcast(I32),
                )

        def load_words(v, queue):
            word_win[v] = keep.tile([P, T], I32, name="word_win", align_bytes=64)
            queue.dma_start(word_win[v][:], words_hbm[v][0].rearrange("p t b -> p (t b)").bitcast(I32))

        def load_wr(a, h, queue):
            wr_raw[a, h] = stage.tile([P, PACK, NH], F32, name="wr_raw")
            rows = wr[512 * a : 512 * (a + 1), NH * h : NH * (h + 1)]
            queue.dma_start(wr_raw[a, h][:], rows.rearrange("(p i) n -> p i n", i=PACK))

        nc.vector.memset(scale_win[IM][:], 0)
        nc.vector.memset(wi_plane[:], 0)
        nc.vector.memset(moved[:], 0)
        nc.vector.memset(scale_win[RE][:], 0)
        zero_in = keep.tile([P, 1], F32, name="zero_in")
        zero = keep.tile([P, 1], F32, name="zero")
        nc.gpsimd.memset(zero_in[:], 0.0)

        def load_wi(a):
            nc.scalar.dma_start(wi_codes[:, a, :], wi_words[a].rearrange("p n i -> p (n i)").bitcast(I32))

        load_words(IM, nc.scalar)
        load_wi(0)
        nc.scalar.activation(zero[:], zero_in[:], ACT.Sqrt)
        load_scales(IM)
        for q in range(4):
            nc.sync.dma_start(
                wi_plane[32 * q : 32 * q + 4, :, :],
                wi_scales[:, 4 * q : 4 * q + 4, :].rearrange("a r n -> r a n").bitcast(I32),
            )
        load_wi(1)
        load_wr(0, 0, nc.scalar)
        load_wr(1, 0, nc.scalar)
        load_scales(RE)

        planes = {}
        codes = {}
        picked = {}

        def gather_scales(v, jt):
            both = keep.tile([P, JT], U8, name="both%d%d" % (v, jt), align_bytes=64)
            lst = offsets[:, jt * (JT // 16) : (jt + 1) * (JT // 16)]
            nc.vector.tensor_copy(both[:], scale_win[v][:].bitcast(U8).indirect(lst))
            dst = moved[:, v, jt * (JT // 4) : (jt + 1) * (JT // 4)]
            nc.sync.dma_start(dst[0:SHIFT_ROWS, :], both[SHIFT : SHIFT + SHIFT_ROWS, :].bitcast(I32))
            planes[v, jt] = [both[:], dst.bitcast(U8)]

        def gather_words(v, jt):
            picked[v, jt] = keep.tile([P, JT], U32, name="picked%d%d" % (v, jt), align_bytes=64)
            lst = offsets[:, jt * (JT // 16) : (jt + 1) * (JT // 16)]
            nc.vector.tensor_copy(picked[v, jt][:], word_win[v][:].bitcast(U32).indirect(lst))

        def part_words(v, jt):
            codes[v, jt] = keep.tile([P, PASSES, 2 * JT], U8, name="codes%d%d" % (v, jt), align_bytes=64)
            nc.vector.tensor_copy(
                codes[v, jt][:].bitcast(U16),
                picked[v, jt][:].bitcast(U16).rearrange("p (j d) -> p d j", d=PASSES),
            )

        hi_bf = {}
        lo_bf = {}
        upper = {}
        wq = {}

        def upper_halves(a, h):
            upper[a, h] = keep.tile([P, NH, PACK], BF16, name="upper%d%d" % (a, h), align_bytes=64)
            halves = wr_raw[a, h][:].bitcast(BF16).rearrange("p i (c n e) -> p c i n e", n=4, e=2)
            nc.scalar.copy(upper[a, h][:].rearrange("p (c n) i -> p c i n", n=4), halves[:, :, :, :, 1])

        def mask_hi(a, h):
            hi_bf[a, h] = keep.tile([P, NH * PACK], BF16, name="hi%d%d" % (a, h), align_bytes=64)
            nc.vector.tensor_scalar(
                hi_bf[a, h][:].bitcast(I32),
                upper[a, h][:].rearrange("p n i -> p (n i)").bitcast(I32),
                HI_MASK,
                None,
                ALU.bitwise_and,
            )

        def make_lo(a, h):
            lo_bf[a, h] = keep.tile([P, NH * PACK], BF16, name="lo%d%d" % (a, h), align_bytes=64)
            nc.vector.tensor_tensor(
                lo_bf[a, h][:].rearrange("p (c n i) -> p c i n", n=4, i=PACK),
                wr_raw[a, h][:].rearrange("p i (c n) -> p c i n", n=4),
                hi_bf[a, h][:].rearrange("p (c n i) -> p c i n", n=4, i=PACK),
                ALU.subtract,
            )

        def quantise(part, a, h):
            src = hi_bf if part == "hi" else lo_bf
            c = keep.tile([P, NH], U32, name="c%s%d%d" % (part, a, h), align_bytes=64)
            s = keep.tile([P, NH], U8, name="s%s%d%d" % (part, a, h), align_bytes=64)
            nc.vector.quantize_mx(c[:].bitcast(FP8X4), s[:], src[a, h][:])
            wq[part, a, h] = (c, s)

        banks = {}
        done = {}
        TOTAL = {"ii": 2, "rr": 4, "ri": 6}

        def mm(group, part, v, a, nt, jt):
            key = (group, nt, jt)
            if key not in banks:
                banks[key] = psum.tile([P, JT], F32, name="acc")
                done[key] = 0
            if part == "wi":
                w = wi_codes[:, a, nt * P : (nt + 1) * P]
                ws = wi_plane[:, a, :].bitcast(U8)[:, nt * P : (nt + 1) * P]
            else:
                c, s = wq[part, a, nt // 2]
                w = c[:, (nt % 2) * P : (nt % 2 + 1) * P]
                ws = s[:, (nt % 2) * P : (nt % 2 + 1) * P]
            nc.tensor.matmul_mx(
                banks[key][:],
                lhsT=w.bitcast(FP8X4),
                lhsT_scale=ws,
                rhs=codes[v, jt][:, a, :].bitcast(FP4X4),
                rhs_scale=planes[v, jt][a],
                start=(done[key] == 0),
                stop=(done[key] == TOTAL[group] - 1),
            )
            done[key] += 1

        ii_sb = {}
        zr_sq = {}

        def take_ii(nt, jt):
            ii_sb[nt, jt] = keep.tile([P, JT], F32, name="ii%d%d" % (nt, jt))
            nc.scalar.copy(ii_sb[nt, jt][:], banks["ii", nt, jt][:])

        def take_rr(nt, jt):
            zr = work.tile([P, JT], F32, name="zr")
            nc.vector.tensor_tensor(zr[:], banks["rr", nt, jt][:], ii_sb[nt, jt][:], ALU.subtract)
            zr_sq[nt, jt] = work.tile([P, JT], F32, name="zr_sq")
            nc.scalar.activation(zr_sq[nt, jt][:], zr[:], ACT.Square)

        zi_sq = {}

        def take_ri(nt, jt, pieces=1):
            zi_sq[nt, jt] = work.tile([P, JT], F32, name="zi_sq")
            w = JT // pieces
            for c in range(0, JT, w):
                nc.scalar.activation(zi_sq[nt, jt][:, c : c + w], banks["ri", nt, jt][:, c : c + w], ACT.Square)

        def finish(nt, jt, pieces=1):
            total = work.tile([P, JT], F32, name="total")
            mag = work.tile([P, JT], F32, name="mag")
            w = JT // pieces
            for c in range(0, JT, w):
                cols = slice(c, c + w)
                nc.vector.tensor_tensor(total[:, cols], zi_sq[nt, jt][:, cols], zr_sq[nt, jt][:, cols], ALU.add)
                nc.scalar.activation(mag[:, cols], total[:, cols], ACT.Sqrt, bias=zero[:])
                nc.sync.dma_start(out[nt * P : (nt + 1) * P, jt * JT + c : jt * JT + c + w], mag[:, cols])

        def ii_tiles(jt):
            for a in range(PASSES):
                for nt in range(4):
                    mm("ii", "wi", IM, a, nt, jt)
            for nt in range(4):
                take_ii(nt, jt)

        def hilo(group, v, a, nt, jt):
            mm(group, "hi", v, a, nt, jt)
            mm(group, "lo", v, a, nt, jt)

        gather_words(IM, 0)
        gather_scales(IM, 0)
        part_words(IM, 0)
        ii_tiles(0)
        upper_halves(0, 0)
        upper_halves(1, 0)
        gather_words(IM, 1)
        load_words(RE, nc.sync)
        gather_scales(IM, 1)
        part_words(IM, 1)
        ii_tiles(1)
        mask_hi(0, 0)
        mask_hi(1, 0)
        make_lo(0, 0)
        load_wr(0, 1, nc.sync)
        quantise("hi", 0, 0)
        quantise("lo", 0, 0)
        make_lo(1, 0)
        load_wr(1, 1, nc.sync)
        quantise("hi", 1, 0)
        quantise("lo", 1, 0)
        for a in range(PASSES):
            for jt in range(2):
                for nt in range(2):
                    hilo("ri", IM, a, nt, jt)
        upper_halves(0, 1)
        upper_halves(1, 1)
        for jt in range(2):
            gather_words(RE, jt)
            gather_scales(RE, jt)
            part_words(RE, jt)
            for a in range(PASSES):
                for nt in range(2):
                    hilo("rr", RE, a, nt, jt)
                    mm("ri", "wi", RE, a, nt, jt)
            if jt == 1:
                mask_hi(0, 1)
                mask_hi(1, 1)
                make_lo(0, 1)
                quantise("hi", 0, 1)
                quantise("lo", 0, 1)
                for nt in range(2):
                    take_rr(nt, 0)
                    take_ri(nt, 0)
                make_lo(1, 1)
                quantise("hi", 1, 1)
                quantise("lo", 1, 1)
        for nt in range(2):
            take_rr(nt, 1)
            take_ri(nt, 1)
        for jt in range(2):
            for nt in range(2):
                finish(nt, jt)
        for jt in range(2):
            for nt in range(2, 4):
                for a in range(PASSES):
                    mm("ri", "wi", RE, a, nt, jt)
        for jt in range(2):
            for nt in range(2, 4):
                pieces = 2 if (jt, nt) == (1, 3) else 1
                for a in range(PASSES):
                    hilo("rr", RE, a, nt, jt)
                for a in range(PASSES):
                    hilo("ri", IM, a, nt, jt)
                take_rr(nt, jt)
                take_ri(nt, jt, pieces)
                finish(nt, jt, pieces)
